import numpy as np, ml_dtypes
CORES = [19,27,51,107,147,155,179,235,275,283,307,363,403,411,435,491]
N = 16
C = 64
SIGN = [[1,1,1,1,1,1,1,1,1,1,1,1,1,1,1,1],[1,-1,1,-1,1,-1,1,-1,1,-1,1,-1,1,-1,1,-1],[1,1,-1,-1,1,1,-1,-1,1,1,-1,-1,1,1,-1,-1],[1,-1,-1,1,1,-1,-1,1,1,-1,-1,1,1,-1,-1,1],[1,1,1,1,-1,-1,-1,-1,1,1,1,1,-1,-1,-1,-1],[1,-1,1,-1,-1,1,-1,1,1,-1,1,-1,-1,1,-1,1],[1,1,-1,-1,-1,-1,1,1,1,1,-1,-1,-1,-1,1,1],[1,-1,-1,1,-1,1,1,-1,1,-1,-1,1,-1,1,1,-1],[1,1,1,1,1,1,1,1,-1,-1,-1,-1,-1,-1,-1,-1],[1,-1,1,-1,1,-1,1,-1,-1,1,-1,1,-1,1,-1,1],[1,1,-1,-1,1,1,-1,-1,-1,-1,1,1,-1,-1,1,1],[1,-1,-1,1,1,-1,-1,1,-1,1,1,-1,-1,1,1,-1],[1,1,1,1,-1,-1,-1,-1,-1,-1,-1,-1,1,1,1,1],[1,-1,1,-1,-1,1,-1,1,-1,1,-1,1,1,-1,1,-1],[1,1,-1,-1,-1,-1,1,1,-1,-1,1,1,1,1,-1,-1],[1,-1,-1,1,-1,1,1,-1,-1,1,1,-1,1,-1,-1,1]]
def setup_inputs(rng):
    return {"x": rng.standard_normal((N, 128, C), dtype=np.float32).astype(ml_dtypes.bfloat16)}
def setup_inputs_big(rng):
    d = setup_inputs(rng)
    for k in ("x",): d[k] = (d[k].astype(np.float32) * 1048576.0).astype(d[k].dtype)
    return d
def setup_inputs_small(rng):
    d = setup_inputs(rng)
    for k in ("x",): d[k] = (d[k].astype(np.float32) * (1 / 1048576.0)).astype(d[k].dtype)
    return d
def setup_inputs_apart(rng):
    d = setup_inputs(rng)
    f = (10.0 ** rng.permutation(np.linspace(-1.5, 1.5, N))).astype(np.float32).reshape(N, 1, 1)
    for k in ("x",): d[k] = (d[k].astype(np.float32) * f).astype(d[k].dtype)
    return d
def reference(x):
    X = x.astype(np.float64)
    y = np.stack([sum(SIGN[r][j] * X[j] for j in range(N)) for r in range(N)])
    return {"y": y.astype(ml_dtypes.bfloat16)}

@@ -1,0 +1,145 @@
+from concourse.bass import DstId, RemoteDMATransfer
+from concourse.mybir import AluOpType
+
+C = 64
+
+SCRATCH = {
+    "xs": ("sbuf", [128, C], "bfloat16"),
+    "la": ("sbuf", [128, 3 * C], "bfloat16"),
+    "tmp": ("sbuf", [128, 6 * C], "bfloat16"),
+    "u": ("sbuf", [128, C], "bfloat16"),
+    "v": ("sbuf", [128, C], "bfloat16"),
+    "lb": ("sbuf", [128, 3 * C], "bfloat16"),
+    "zero": ("sbuf", [128, C], "bfloat16"),
+    "out": ("sbuf", [128, C], "bfloat16"),
+}
+SEMAPHORES = (["ld", "st", "sent", "zf"] + ["a%d" % i for i in range(4)] + ["b%d" % i for i in range(4)]
+              + ["c%d" % i for i in range(10)])
+
+
+def _one_link(topo, a, b):
+    if topo.mates(a, b) or topo.same_plane(a, b):
+        return True
+    return topo.rack(topo.host(a)) != topo.rack(topo.host(b)) and topo.chip(a) == topo.chip(b)
+
+
+def _groups(T, topo):
+    cores = T.cores
+    n = len(cores)
+    da = [j for j in range(1, n) if topo.same_plane(cores[0], cores[j])]
+    best = None
+    for b1 in range(1, n):
+        for b2 in range(b1 + 1, n):
+            db = [b1, b2, b1 ^ b2]
+            if (b1 ^ b2) < b2 or [b for b in db if b in da]:
+                continue
+            pairs = [(cores[r], cores[r ^ b]) for r in range(n) for b in db]
+            if not all(topo.may_write(s, d) for s, d in pairs):
+                continue
+            score = sum(1 for s, d in pairs if _one_link(topo, s, d))
+            if best is None or score > best[0]:
+                best = (score, db)
+    return da, best[1]
+
+
+def _engines(topo, core, dsts):
+    m = topo.mask(core, dsts[0])
+    for d in dsts[1:]:
+        m &= topo.mask(core, d)
+    return m, bin(m).count("1")
+
+
+def rank_program(g, core, T, topo):
+    r = T.rank_of(core)
+    if r is None:
+        return
+    sign = T.tables["SIGN"]
+    cores = T.cores
+    da, db = _groups(T, topo)
+    far = [b for b in db if [a for a in da if sign[b][a] < 0]]
+    near = [b for b in db if b not in far]
+    split = [a for a in da if sign[far[0]][a] < 0]
+    da = [a for a in da if a not in split] + split
+    db = far + near
+
+    def place(s, grp):
+        return sorted([s] + [s ^ d for d in grp]).index(s)
+
+    def tile(buf, k):
+        return buf[:, k * C:(k + 1) * C]
+
+    def send(src, land, slot_of, grp, ds, sem_name):
+        dsts = [cores[r ^ d] for d in ds]
+        mask, _ = _engines(topo, core, dsts)
+        ids = [topo.addr(d, core) for d in dsts]
+        g.remote_dma_fused([RemoteDMATransfer(
+            dst_ids=[DstId(rid=rid, pnc=pid) for rid, pid in ids], dma_engine_mask=mask,
+            remote_sem=T.sem["%s%d" % (sem_name, place(r, grp))],
+            srcs=[src], dsts=[tile(land, slot_of.index(d)) for d in ds], alu_op=0)], local_sem=T.sem.sent)
+        return _engines(topo, core, dsts)[1]
+
+    def landed(d, grp, sem_name):
+        s = r ^ d
+        batch = [e for e in grp if (e in far) == (d in far)] if grp is db else grp
+        return T.sem["%s%d" % (sem_name, place(s, grp))], _engines(topo, cores[s], [cores[s ^ e] for e in batch])[1]
+
+    seen = []
+    count = [0, 0]
+
+    def vop(out, in0, in1, op, waits):
+        for w in waits:
+            if w not in seen:
+                g.vector.wait_ge(w[0], w[1])
+                seen.append(w)
+        sem = T.sem["c%d" % count[0]]
+        count[0] += 1
+        g.vector.tensor_tensor(out=out, in0=in0, in1=in1, op=op).then_inc(sem, 1)
+        return (sem, 1)
+
+    def fresh():
+        count[1] += 1
+        return tile(T.tmp, count[1] - 1)
+
+    def add(out, acc, term, s):
+        return out, vop(out, acc[0], term[0], AluOpType.add if s > 0 else AluOpType.subtract, [acc[1], term[1]])
+
+    g.sync.dma_start(out=T.xs[:, :], in_=T.x[:, :]).then_inc(T.sem.ld, 16)
+    g.wait_ge(T.sem.ld, 16)
+    left = send(T.xs[:, :], T.la, da, da, da, "a")
+
+    pat_u = sign[r]
+    pat_v = sign[r ^ far[0]]
+    got = [(tile(T.la, k), landed(a, da, "a")) for k, a in enumerate(da)]
+    acc_u = acc_v = (T.xs[:, :], (T.sem.ld, 16))
+    for k, a in enumerate(da):
+        last = k == len(da) - 1
+        if a not in split:
+            acc_u = acc_v = add(fresh(), acc_u, got[k], pat_u[a])
+        else:
+            acc_v = add(T.v[:, :] if last else fresh(), acc_v, got[k], pat_v[a])
+            acc_u = add(T.u[:, :] if last else fresh(), acc_u, got[k], pat_u[a])
+
+    g.wait_ge(acc_v[1][0], acc_v[1][1])
+    left += send(T.v[:, :], T.lb, db, db, far, "b")
+    g.wait_ge(acc_u[1][0], acc_u[1][1])
+    left += send(T.u[:, :], T.lb, db, db, near, "b")
+
+    acc, neg = acc_u, sign[r][r] < 0
+    if neg and all(sign[r][r ^ b] < 0 for b in db):
+        g.vector.memset(T.zero[:, :], 0.0).then_inc(T.sem.zf, 1)
+        acc, neg = add(fresh(), (T.zero[:, :], (T.sem.zf, 1)), acc, -1), False
+    for k, b in enumerate(db):
+        out = T.out[:, :] if k == len(db) - 1 else fresh()
+        term = (tile(T.lb, k), landed(b, db, "b"))
+        s = sign[r][r ^ b]
+        if not neg:
+            acc = add(out, acc, term, s)
+        elif s > 0:
+            acc, neg = add(out, term, acc, -1), False
+        else:
+            acc = add(out, acc, term, 1)
+
+    g.sync.wait_ge(acc[1][0], acc[1][1])
+    g.sync.dma_start(out=T.y[:, :], in_=T.out[:, :]).then_inc(T.sem.st, 16)
+    g.sync.wait_ge(T.sem.st, 16)
+    g.wait_ge(T.sem.sent, left)

@@ -6,40 +6,47 @@ C = 64
 SCRATCH = {
     "xs": ("sbuf", [128, C], "bfloat16"),
     "la": ("sbuf", [128, 3 * C], "bfloat16"),
-    "tmp": ("sbuf", [128, 6 * C], "bfloat16"),
+    "lx": ("sbuf", [128, C], "bfloat16"),
+    "tmp": ("sbuf", [128, 10 * C], "bfloat16"),
     "u": ("sbuf", [128, C], "bfloat16"),
     "v": ("sbuf", [128, C], "bfloat16"),
     "lb": ("sbuf", [128, 3 * C], "bfloat16"),
     "zero": ("sbuf", [128, C], "bfloat16"),
     "out": ("sbuf", [128, C], "bfloat16"),
 }
-SEMAPHORES = (["ld", "st", "sent", "zf"] + ["a%d" % i for i in range(4)] + ["b%d" % i for i in range(4)]
-              + ["c%d" % i for i in range(10)])
+SEMAPHORES = (["ld", "st", "sent", "zf", "e0"] + ["a%d" % i for i in range(4)] + ["b%d" % i for i in range(4)]
+              + ["c%d" % i for i in range(14)])
 
 
-def _one_link(topo, a, b):
-    if topo.mates(a, b) or topo.same_plane(a, b):
-        return True
-    return topo.rack(topo.host(a)) != topo.rack(topo.host(b)) and topo.chip(a) == topo.chip(b)
+def _links(topo, cores, a, b):
+    h = 0
+    if topo.rack(topo.host(a)) != topo.rack(topo.host(b)):
+        h = 1
+        b = [c for c in cores if topo.host(c) == topo.host(a) and topo.chip(c) == topo.chip(b)][0]
+    if a == b:
+        return h
+    return h + (1 if topo.mates(a, b) or topo.same_plane(a, b) else 2)
 
 
 def _groups(T, topo):
     cores = T.cores
+    sign = T.tables["SIGN"]
     n = len(cores)
-    da = [j for j in range(1, n) if topo.same_plane(cores[0], cores[j])]
+    ok = [d for d in range(1, n) if all(topo.may_write(cores[r], cores[r ^ d]) for r in range(n))]
+    each = dict((d, [_links(topo, cores, cores[r], cores[r ^ d]) for r in range(n)]) for d in ok)
+    subs = [[p, q, p ^ q] for p in ok for q in ok if p < q < (p ^ q) and (p ^ q) in ok]
     best = None
-    for b1 in range(1, n):
-        for b2 in range(b1 + 1, n):
-            db = [b1, b2, b1 ^ b2]
-            if (b1 ^ b2) < b2 or [b for b in db if b in da]:
+    for ga in subs:
+        if not [a for a in ga if topo.rack(topo.host(cores[0])) != topo.rack(topo.host(cores[a]))]:
+            continue
+        for gb in subs:
+            if len(set(a ^ b for a in [0] + ga for b in [0] + gb)) < n:
                 continue
-            pairs = [(cores[r], cores[r ^ b]) for r in range(n) for b in db]
-            if not all(topo.may_write(s, d) for s, d in pairs):
-                continue
-            score = sum(1 for s, d in pairs if _one_link(topo, s, d))
-            if best is None or score > best[0]:
-                best = (score, db)
-    return da, best[1]
+            kinds = len(set(tuple(sign[b][a] for a in ga) for b in [0] + gb))
+            score = (max(max(each[d]) for d in ga + gb), kinds, sum(sum(each[d]) for d in ga + gb))
+            if best is None or score < best[0]:
+                best = (score, ga, gb)
+    return best[1], best[2], dict((d, sum(each[d])) for d in ok)
 
 
 def _engines(topo, core, dsts):
@@ -55,12 +62,12 @@ def rank_program(g, core, T, topo):
         return
     sign = T.tables["SIGN"]
     cores = T.cores
-    da, db = _groups(T, topo)
-    far = [b for b in db if [a for a in da if sign[b][a] < 0]]
-    near = [b for b in db if b not in far]
-    split = [a for a in da if sign[far[0]][a] < 0]
-    da = [a for a in da if a not in split] + split
-    db = far + near
+    da, db, way = _groups(T, topo)
+    other = sorted([b for b in db if [a for a in da if sign[b][a] < 0]], key=lambda d: -way[d])
+    same = [b for b in db if b not in other]
+    da = sorted(da, key=lambda d: (-way[d], topo.same_plane(cores[0], cores[d])))
+    db = same + other
+    direct = da[-1] ^ same[0]
 
     def place(s, grp):
         return sorted([s] + [s ^ d for d in grp]).index(s)
@@ -68,70 +75,67 @@ def rank_program(g, core, T, topo):
     def tile(buf, k):
         return buf[:, k * C:(k + 1) * C]
 
-    def send(src, land, slot_of, grp, ds, sem_name):
+    def send(src, lands, ds, sem):
         dsts = [cores[r ^ d] for d in ds]
-        mask, _ = _engines(topo, core, dsts)
+        mask, k = _engines(topo, core, dsts)
         ids = [topo.addr(d, core) for d in dsts]
         g.remote_dma_fused([RemoteDMATransfer(
-            dst_ids=[DstId(rid=rid, pnc=pid) for rid, pid in ids], dma_engine_mask=mask,
-            remote_sem=T.sem["%s%d" % (sem_name, place(r, grp))],
-            srcs=[src], dsts=[tile(land, slot_of.index(d)) for d in ds], alu_op=0)], local_sem=T.sem.sent)
-        return _engines(topo, core, dsts)[1]
+            dst_ids=[DstId(rid=rid, pnc=pid) for rid, pid in ids], dma_engine_mask=mask, remote_sem=sem,
+            srcs=[src], dsts=lands, alu_op=0)], local_sem=T.sem.sent)
+        return k
 
-    def landed(d, grp, sem_name):
+    def landed(d, batch, sem):
         s = r ^ d
-        batch = [e for e in grp if (e in far) == (d in far)] if grp is db else grp
-        return T.sem["%s%d" % (sem_name, place(s, grp))], _engines(topo, cores[s], [cores[s ^ e] for e in batch])[1]
+        return sem, _engines(topo, cores[s], [cores[s ^ e] for e in batch])[1]
 
     seen = []
     count = [0, 0]
-
-    def vop(out, in0, in1, op, waits):
-        for w in waits:
-            if w not in seen:
-                g.vector.wait_ge(w[0], w[1])
-                seen.append(w)
-        sem = T.sem["c%d" % count[0]]
-        count[0] += 1
-        g.vector.tensor_tensor(out=out, in0=in0, in1=in1, op=op).then_inc(sem, 1)
-        return (sem, 1)
 
     def fresh():
         count[1] += 1
         return tile(T.tmp, count[1] - 1)
 
     def add(out, acc, term, s):
-        return out, vop(out, acc[0], term[0], AluOpType.add if s > 0 else AluOpType.subtract, [acc[1], term[1]])
+        for w in (acc[1], term[1]):
+            if w not in seen:
+                g.vector.wait_ge(w[0], w[1])
+                seen.append(w)
+        sem = T.sem["c%d" % count[0]]
+        count[0] += 1
+        g.vector.tensor_tensor(out=out, in0=acc[0], in1=term[0],
+                               op=AluOpType.add if s > 0 else AluOpType.subtract).then_inc(sem, 1)
+        return out, (sem, 1)
 
     g.sync.dma_start(out=T.xs[:, :], in_=T.x[:, :]).then_inc(T.sem.ld, 16)
     g.wait_ge(T.sem.ld, 16)
-    left = send(T.xs[:, :], T.la, da, da, da, "a")
+    left = send(T.xs[:, :], [tile(T.la, k) for k in range(len(da))], da, T.sem["a%d" % place(r, da)])
+    left += send(T.xs[:, :], [T.lx[:, :]], [direct], T.sem.e0)
 
     pat_u = sign[r]
-    pat_v = sign[r ^ far[0]]
-    got = [(tile(T.la, k), landed(a, da, "a")) for k, a in enumerate(da)]
+    pat_v = sign[r ^ other[0]]
+    got = [(tile(T.la, k), landed(a, da, T.sem["a%d" % place(r ^ a, da)])) for k, a in enumerate(da)]
     acc_u = acc_v = (T.xs[:, :], (T.sem.ld, 16))
-    for k, a in enumerate(da):
-        last = k == len(da) - 1
-        if a not in split:
-            acc_u = acc_v = add(fresh(), acc_u, got[k], pat_u[a])
-        else:
-            acc_v = add(T.v[:, :] if last else fresh(), acc_v, got[k], pat_v[a])
-            acc_u = add(T.u[:, :] if last else fresh(), acc_u, got[k], pat_u[a])
+    for k, a in enumerate(da[:-1]):
+        acc_u = add(fresh(), acc_u, got[k], pat_u[a])
+        acc_v = add(fresh(), acc_v, got[k], pat_v[a])
 
-    g.wait_ge(acc_v[1][0], acc_v[1][1])
-    left += send(T.v[:, :], T.lb, db, db, far, "b")
     g.wait_ge(acc_u[1][0], acc_u[1][1])
-    left += send(T.u[:, :], T.lb, db, db, near, "b")
+    left += send(acc_u[0], [tile(T.lb, 0)], same, T.sem["b%d" % place(r, db)])
+    acc_v = add(T.v[:, :], acc_v, got[-1], pat_v[da[-1]])
+    acc_u = add(T.u[:, :], acc_u, got[-1], pat_u[da[-1]])
+    g.wait_ge(acc_v[1][0], acc_v[1][1])
+    left += send(T.v[:, :], [tile(T.lb, db.index(b)) for b in other], other, T.sem["b%d" % place(r, db)])
 
+    terms = [((T.lx[:, :], landed(direct, [direct], T.sem.e0)), sign[r][r ^ direct])]
+    for k, b in enumerate(db):
+        batch = other if b in other else same
+        terms.append(((tile(T.lb, k), landed(b, batch, T.sem["b%d" % place(r ^ b, db)])), sign[r][r ^ b]))
     acc, neg = acc_u, sign[r][r] < 0
-    if neg and all(sign[r][r ^ b] < 0 for b in db):
+    if neg and all(s < 0 for _, s in terms):
         g.vector.memset(T.zero[:, :], 0.0).then_inc(T.sem.zf, 1)
         acc, neg = add(fresh(), (T.zero[:, :], (T.sem.zf, 1)), acc, -1), False
-    for k, b in enumerate(db):
-        out = T.out[:, :] if k == len(db) - 1 else fresh()
-        term = (tile(T.lb, k), landed(b, db, "b"))
-        s = sign[r][r ^ b]
+    for k, (term, s) in enumerate(terms):
+        out = T.out[:, :] if k == len(terms) - 1 else fresh()
         if not neg:
             acc = add(out, acc, term, s)
         elif s > 0:

from concourse.bass import DstId, RemoteDMATransfer
from concourse.mybir import AluOpType

C = 64

SCRATCH = {
    "xs": ("sbuf", [128, C], "bfloat16"),
    "la": ("sbuf", [128, 3 * C], "bfloat16"),
    "lx": ("sbuf", [128, C], "bfloat16"),
    "tmp": ("sbuf", [128, 10 * C], "bfloat16"),
    "u": ("sbuf", [128, C], "bfloat16"),
    "v": ("sbuf", [128, C], "bfloat16"),
    "lb": ("sbuf", [128, 3 * C], "bfloat16"),
    "zero": ("sbuf", [128, C], "bfloat16"),
    "out": ("sbuf", [128, C], "bfloat16"),
}
SEMAPHORES = (["ld", "st", "sent", "zf", "e0"] + ["a%d" % i for i in range(4)] + ["b%d" % i for i in range(4)]
              + ["c%d" % i for i in range(14)])


def _links(topo, cores, a, b):
    h = 0
    if topo.rack(topo.host(a)) != topo.rack(topo.host(b)):
        h = 1
        b = [c for c in cores if topo.host(c) == topo.host(a) and topo.chip(c) == topo.chip(b)][0]
    if a == b:
        return h
    return h + (1 if topo.mates(a, b) or topo.same_plane(a, b) else 2)


def _groups(T, topo):
    cores = T.cores
    sign = T.tables["SIGN"]
    n = len(cores)
    ok = [d for d in range(1, n) if all(topo.may_write(cores[r], cores[r ^ d]) for r in range(n))]
    each = dict((d, [_links(topo, cores, cores[r], cores[r ^ d]) for r in range(n)]) for d in ok)
    subs = [[p, q, p ^ q] for p in ok for q in ok if p < q < (p ^ q) and (p ^ q) in ok]
    best = None
    for ga in subs:
        if not [a for a in ga if topo.rack(topo.host(cores[0])) != topo.rack(topo.host(cores[a]))]:
            continue
        for gb in subs:
            if len(set(a ^ b for a in [0] + ga for b in [0] + gb)) < n:
                continue
            kinds = len(set(tuple(sign[b][a] for a in ga) for b in [0] + gb))
            score = (max(max(each[d]) for d in ga + gb), kinds, sum(sum(each[d]) for d in ga + gb))
            if best is None or score < best[0]:
                best = (score, ga, gb)
    return best[1], best[2], dict((d, sum(each[d])) for d in ok)


def _engines(topo, core, dsts):
    m = topo.mask(core, dsts[0])
    for d in dsts[1:]:
        m &= topo.mask(core, d)
    return m, bin(m).count("1")


def rank_program(g, core, T, topo):
    r = T.rank_of(core)
    if r is None:
        return
    sign = T.tables["SIGN"]
    cores = T.cores
    da, db, way = _groups(T, topo)
    other = sorted([b for b in db if [a for a in da if sign[b][a] < 0]], key=lambda d: -way[d])
    same = [b for b in db if b not in other]
    da = sorted(da, key=lambda d: (-way[d], topo.same_plane(cores[0], cores[d])))
    db = same + other
    direct = da[-1] ^ same[0]

    def place(s, grp):
        return sorted([s] + [s ^ d for d in grp]).index(s)

    def tile(buf, k):
        return buf[:, k * C:(k + 1) * C]

    def send(src, lands, ds, sem):
        dsts = [cores[r ^ d] for d in ds]
        mask, k = _engines(topo, core, dsts)
        ids = [topo.addr(d, core) for d in dsts]
        g.remote_dma_fused([RemoteDMATransfer(
            dst_ids=[DstId(rid=rid, pnc=pid) for rid, pid in ids], dma_engine_mask=mask, remote_sem=sem,
            srcs=[src], dsts=lands, alu_op=0)], local_sem=T.sem.sent)
        return k

    def landed(d, batch, sem):
        s = r ^ d
        return sem, _engines(topo, cores[s], [cores[s ^ e] for e in batch])[1]

    seen = []
    count = [0, 0]

    def fresh():
        count[1] += 1
        return tile(T.tmp, count[1] - 1)

    def add(out, acc, term, s):
        for w in (acc[1], term[1]):
            if w not in seen:
                g.vector.wait_ge(w[0], w[1])
                seen.append(w)
        sem = T.sem["c%d" % count[0]]
        count[0] += 1
        g.vector.tensor_tensor(out=out, in0=acc[0], in1=term[0],
                               op=AluOpType.add if s > 0 else AluOpType.subtract).then_inc(sem, 1)
        return out, (sem, 1)

    g.sync.dma_start(out=T.xs[:, :], in_=T.x[:, :]).then_inc(T.sem.ld, 16)
    g.wait_ge(T.sem.ld, 16)
    left = send(T.xs[:, :], [tile(T.la, k) for k in range(len(da))], da, T.sem["a%d" % place(r, da)])
    left += send(T.xs[:, :], [T.lx[:, :]], [direct], T.sem.e0)

    pat_u = sign[r]
    pat_v = sign[r ^ other[0]]
    got = [(tile(T.la, k), landed(a, da, T.sem["a%d" % place(r ^ a, da)])) for k, a in enumerate(da)]
    acc_u = acc_v = (T.xs[:, :], (T.sem.ld, 16))
    for k, a in enumerate(da[:-1]):
        acc_u = add(fresh(), acc_u, got[k], pat_u[a])
        acc_v = add(fresh(), acc_v, got[k], pat_v[a])

    g.wait_ge(acc_u[1][0], acc_u[1][1])
    left += send(acc_u[0], [tile(T.lb, 0)], same, T.sem["b%d" % place(r, db)])
    acc_v = add(T.v[:, :], acc_v, got[-1], pat_v[da[-1]])
    acc_u = add(T.u[:, :], acc_u, got[-1], pat_u[da[-1]])
    g.wait_ge(acc_v[1][0], acc_v[1][1])
    left += send(T.v[:, :], [tile(T.lb, db.index(b)) for b in other], other, T.sem["b%d" % place(r, db)])

    terms = [((T.lx[:, :], landed(direct, [direct], T.sem.e0)), sign[r][r ^ direct])]
    for k, b in enumerate(db):
        batch = other if b in other else same
        terms.append(((tile(T.lb, k), landed(b, batch, T.sem["b%d" % place(r ^ b, db)])), sign[r][r ^ b]))
    acc, neg = acc_u, sign[r][r] < 0
    if neg and all(s < 0 for _, s in terms):
        g.vector.memset(T.zero[:, :], 0.0).then_inc(T.sem.zf, 1)
        acc, neg = add(fresh(), (T.zero[:, :], (T.sem.zf, 1)), acc, -1), False
    for k, (term, s) in enumerate(terms):
        out = T.out[:, :] if k == len(terms) - 1 else fresh()
        if not neg:
            acc = add(out, acc, term, s)
        elif s > 0:
            acc, neg = add(out, term, acc, -1), False
        else:
            acc = add(out, acc, term, 1)

    g.sync.wait_ge(acc[1][0], acc[1][1])
    g.sync.dma_start(out=T.y[:, :], in_=T.out[:, :]).then_inc(T.sem.st, 16)
    g.sync.wait_ge(T.sem.st, 16)
    g.wait_ge(T.sem.sent, left)
